import numpy as np, ml_dtypes
CORES = [33,38,57,62,81,86,161,166,185,190,209,214]
N = 12
TOK, K = 256, 3
ROUTE = [[[1,2,6],[1,3,11],[3,8,9],[7,8,11],[4,9,10],[4,5,7],[5,6,7],[5,7,10],[3,10,11],[0,3,8],[3,8,10],[7,8,11],[1,3,5],[1,6,8],[2,9,10],[2,4,6],[0,3,4],[2,6,10],[3,6,8],[0,4,10],[3,6,11],[0,2,5],[3,6,9],[4,5,8],[4,7,10],[2,6,11],[1,10,11],[1,9,10],[3,5,7],[3,4,11],[0,7,10],[0,1,6],[2,3,9],[2,4,7],[2,7,11],[2,3,10],[1,5,8],[0,5,10],[2,5,6],[1,5,8],[0,5,10],[0,4,5],[3,8,10],[1,6,11],[0,5,9],[1,3,8],[4,6,8],[0,7,9],[0,7,9],[7,8,11],[1,7,11],[2,8,9],[0,3,8],[4,7,9],[1,6,7],[1,2,3],[3,8,11],[5,8,9],[0,2,3],[1,7,11],[3,4,6],[0,9,10],[2,3,9],[1,8,9],[4,8,10],[1,3,10],[2,3,7],[4,9,11],[1,6,7],[8,9,11],[2,3,5],[5,9,11],[1,3,8],[1,4,6],[5,6,9],[3,4,6],[2,9,11],[6,7,10],[0,9,11],[6,8,9],[0,3,10],[0,7,11],[6,8,9],[1,9,10],[5,7,11],[5,6,8],[5,6,7],[0,6,11],[3,8,9],[0,2,5],[4,5,11],[6,8,9],[5,6,8],[3,9,11],[4,8,11],[2,7,9],[2,9,11],[1,5,11],[3,5,11],[0,5,8],[1,7,11],[3,6,10],[3,6,8],[1,3,9],[2,4,6],[6,8,9],[2,4,7],[3,6,7],[2,7,9],[5,6,8],[1,6,7],[4,5,11],[1,2,5],[1,8,11],[4,6,8],[6,9,11],[0,1,5],[0,5,10],[7,8,9],[3,10,11],[5,7,8],[1,2,3],[0,4,5],[0,3,11],[1,2,9],[1,3,11],[1,2,5],[7,9,11],[7,8,11],[5,6,10],[4,5,10],[3,7,8],[0,3,4],[1,6,9],[1,5,9],[2,3,6],[0,7,11],[0,2,8],[5,8,11],[2,5,9],[3,4,6],[2,3,5],[0,2,5],[5,6,9],[5,6,11],[0,8,11],[0,5,11],[0,5,8],[1,2,6],[2,6,8],[0,6,9],[2,6,11],[0,2,7],[0,7,9],[0,4,6],[6,7,8],[1,4,6],[0,2,9],[0,2,6],[3,8,10],[0,1,5],[0,2,5],[0,2,8],[2,9,10],[0,2,10],[0,6,7],[0,6,10],[0,4,6],[2,3,5],[1,7,11],[7,9,10],[3,8,9],[5,10,11],[3,10,11],[1,8,11],[1,7,11],[5,6,11],[5,9,10],[5,7,11],[0,3,11],[1,5,10],[0,5,9],[0,1,8],[0,5,10],[0,3,5],[1,2,11],[0,2,3],[1,2,3],[1,3,5],[4,6,11],[2,5,9],[1,6,7],[1,7,11],[1,7,11],[0,7,8],[5,7,8],[2,3,5],[4,7,8],[4,8,10],[0,2,7],[6,7,9],[7,9,10],[9,10,11],[6,8,9],[8,9,10],[0,1,11],[1,4,7],[6,10,11],[1,2,7],[7,10,11],[7,8,10],[1,5,11],[1,4,7],[1,9,11],[1,4,6],[5,7,9],[3,6,7],[3,4,10],[0,3,7],[2,6,7],[1,6,11],[2,7,11],[2,3,8],[0,2,7],[4,6,9],[3,7,11],[6,10,11],[0,4,5],[0,1,4],[3,4,11],[1,2,9],[0,7,11],[0,6,9],[5,6,11],[1,6,7],[2,6,10],[0,3,5],[3,7,11],[0,9,10],[0,6,10],[1,7,8],[2,4,6],[2,4,6],[0,2,6],[1,5,8],[1,3,5],[3,5,7],[5,8,11],[1,3,6],[7,10,11],[4,6,7],[2,5,10],[0,5,8],[0,9,10],[2,3,8],[0,9,10]],[[2,4,10],[3,5,9],[4,10,11],[3,7,9],[2,3,4],[2,6,10],[5,7,9],[8,9,10],[0,6,8],[0,5,10],[2,6,8],[2,4,5],[5,9,10],[8,10,11],[0,5,6],[0,1,2],[1,8,9],[6,7,11],[4,5,8],[2,6,8],[4,5,11],[6,9,11],[2,4,7],[4,6,10],[8,9,11],[2,9,11],[0,6,10],[0,2,9],[0,2,7],[2,7,9],[6,7,9],[4,7,11],[0,10,11],[2,3,11],[1,5,7],[2,6,7],[2,8,11],[0,2,6],[0,6,8],[4,6,7],[4,5,8],[4,7,10],[1,3,11],[0,4,11],[6,7,8],[0,2,8],[0,4,6],[0,6,8],[1,4,10],[1,6,7],[0,2,8],[6,9,11],[0,8,10],[5,8,10],[0,4,8],[4,6,11],[3,4,11],[3,6,9],[0,1,2],[0,6,10],[1,3,11],[0,1,5],[0,1,9],[2,3,8],[2,9,10],[0,2,11],[3,4,5],[1,4,9],[2,3,5],[4,7,10],[1,6,8],[3,7,11],[4,7,9],[3,4,10],[4,7,8],[2,5,11],[0,5,6],[3,6,8],[2,4,11],[3,8,9],[0,4,9],[2,4,7],[2,8,9],[6,8,11],[0,3,9],[1,9,11],[1,5,11],[1,10,11],[0,6,10],[5,7,9],[0,6,9],[0,4,10],[2,4,9],[1,4,6],[0,1,7],[5,7,8],[0,4,10],[0,1,2],[0,2,11],[1,2,7],[0,9,11],[0,3,4],[0,3,11],[1,6,10],[0,9,11],[4,5,9],[1,6,10],[4,6,9],[0,3,7],[0,2,5],[5,7,9],[2,4,8],[2,3,10],[3,5,9],[3,5,6],[3,7,8],[4,5,7],[0,1,9],[7,8,11],[5,6,7],[1,8,10],[1,7,8],[1,2,11],[0,1,7],[0,9,11],[2,5,11],[1,5,7],[0,1,4],[2,5,10],[5,6,9],[3,6,11],[1,3,6],[0,7,9],[0,1,2],[2,6,10],[1,6,10],[5,6,11],[4,7,11],[0,3,6],[0,1,5],[2,5,6],[1,2,10],[0,5,11],[5,10,11],[5,7,9],[2,7,10],[0,8,11],[6,7,9],[2,5,7],[4,7,11],[0,1,7],[0,1,8],[2,5,9],[0,1,11],[5,8,11],[4,8,11],[5,8,10],[1,8,10],[6,7,10],[5,9,11],[1,8,9],[0,2,8],[4,9,10],[1,4,9],[6,10,11],[0,1,2],[7,8,9],[2,4,5],[0,3,5],[0,3,8],[2,3,5],[4,5,11],[0,1,6],[2,3,10],[4,5,11],[5,8,10],[0,9,11],[2,6,7],[0,7,8],[7,8,9],[3,4,6],[6,10,11],[3,7,11],[1,2,4],[2,6,10],[7,8,10],[0,1,11],[1,9,10],[5,10,11],[2,6,9],[4,6,8],[4,5,6],[2,3,9],[1,2,11],[3,7,9],[0,5,11],[0,5,9],[3,4,10],[3,5,6],[1,3,11],[3,4,5],[1,2,5],[2,8,11],[0,1,3],[1,3,6],[3,5,11],[3,4,11],[0,6,8],[1,5,10],[4,6,7],[1,3,11],[6,8,10],[0,2,11],[2,6,8],[0,5,8],[2,6,8],[0,4,6],[1,7,8],[3,5,10],[3,5,11],[0,1,7],[5,7,11],[1,2,9],[5,6,11],[4,8,9],[3,6,8],[3,6,9],[1,5,7],[2,8,9],[0,5,11],[3,4,8],[4,7,9],[0,1,11],[0,5,6],[0,2,8],[6,8,9],[1,4,7],[5,7,9],[3,4,8],[1,4,9],[7,9,11],[0,6,7],[2,4,5],[0,7,10],[0,6,8],[2,5,7],[0,2,4],[0,1,5],[0,1,9],[4,8,9],[7,9,10],[2,6,9],[2,5,7],[6,8,10],[1,2,7],[2,4,11]],[[2,9,11],[0,6,10],[2,5,9],[6,7,10],[6,7,9],[3,6,10],[0,1,2],[5,7,9],[1,2,5],[1,6,10],[1,8,11],[0,6,10],[1,3,8],[2,7,9],[7,8,9],[8,10,11],[0,10,11],[0,8,9],[4,5,9],[0,6,7],[3,5,10],[1,4,7],[6,9,11],[0,4,9],[2,7,9],[3,5,7],[2,3,10],[8,9,11],[0,5,10],[6,9,11],[4,5,10],[1,3,8],[5,9,10],[0,9,11],[2,8,11],[2,7,11],[2,8,10],[3,4,9],[3,4,8],[2,6,8],[4,5,10],[0,5,6],[0,5,10],[1,2,11],[3,6,8],[1,5,10],[6,9,11],[0,1,7],[1,3,6],[1,3,7],[2,4,10],[2,6,9],[0,7,11],[2,9,11],[4,7,10],[2,6,11],[6,7,10],[1,3,11],[6,8,11],[0,5,8],[0,4,8],[0,10,11],[0,7,10],[1,4,7],[1,3,5],[0,1,4],[0,4,6],[2,4,6],[3,4,8],[3,5,10],[0,10,11],[2,8,10],[1,7,8],[6,8,11],[0,4,6],[0,4,8],[4,5,6],[3,4,7],[6,8,9],[0,1,7],[1,3,11],[4,7,11],[1,5,7],[2,4,9],[2,9,10],[1,5,6],[7,9,11],[0,3,4],[2,10,11],[2,8,10],[1,2,11],[2,3,7],[1,7,8],[4,5,10],[0,8,11],[1,5,11],[0,3,11],[2,5,11],[4,7,11],[4,6,9],[0,8,11],[1,5,9],[0,6,7],[1,9,10],[4,8,11],[1,6,8],[0,8,11],[1,2,10],[4,6,7],[0,6,11],[0,2,7],[2,6,11],[3,6,8],[4,8,10],[3,10,11],[8,9,10],[4,6,11],[1,4,6],[4,5,9],[4,6,9],[1,5,11],[3,4,7],[2,4,9],[2,6,11],[0,8,9],[2,8,11],[5,9,10],[7,9,10],[9,10,11],[4,8,10],[3,7,9],[0,10,11],[1,4,9],[1,5,7],[3,6,10],[1,2,7],[1,5,7],[3,5,9],[1,5,9],[4,7,11],[3,5,9],[0,6,9],[1,2,10],[3,4,11],[4,9,10],[0,3,4],[0,1,6],[2,8,11],[2,8,11],[0,2,6],[0,2,9],[6,7,10],[1,2,8],[0,1,2],[4,5,6],[6,7,11],[9,10,11],[1,9,11],[1,6,9],[2,3,5],[1,4,9],[0,5,6],[0,7,9],[0,4,6],[5,7,8],[2,6,11],[4,7,9],[1,2,9],[0,9,10],[0,3,11],[2,5,8],[0,4,5],[7,8,11],[4,5,7],[0,4,10],[3,6,9],[1,3,5],[2,6,8],[0,3,11],[1,10,11],[3,9,10],[1,10,11],[1,6,9],[0,1,4],[1,2,7],[0,2,7],[4,7,11],[3,9,10],[2,4,6],[1,3,8],[1,2,6],[2,3,9],[2,6,8],[5,10,11],[0,7,11],[1,3,5],[3,4,7],[4,5,9],[1,5,7],[0,1,3],[1,4,9],[1,6,9],[3,7,11],[2,6,11],[1,2,8],[0,4,8],[0,1,9],[1,8,10],[2,6,10],[2,5,6],[2,9,10],[8,9,11],[2,4,8],[1,2,10],[1,4,9],[1,2,10],[1,2,3],[3,4,6],[3,4,7],[3,4,8],[3,8,11],[3,7,8],[8,9,11],[4,5,6],[1,8,10],[2,4,5],[3,7,11],[2,8,11],[5,6,11],[2,4,8],[0,3,10],[4,5,9],[4,5,9],[3,4,9],[0,7,8],[1,3,8],[5,8,9],[5,6,10],[0,4,6],[2,4,10],[2,6,7],[5,10,11],[0,1,9],[1,2,11],[1,3,9],[4,10,11],[3,7,10],[1,2,10],[4,9,11],[2,4,10],[3,8,9],[3,4,11],[1,4,7],[0,5,10],[1,4,6],[2,8,9]],[[0,3,10],[2,3,7],[4,9,11],[1,2,8],[4,6,7],[3,6,10],[1,6,10],[6,10,11],[4,8,11],[4,5,11],[3,7,9],[0,2,5],[4,5,6],[4,5,11],[0,2,6],[3,4,6],[2,5,6],[2,6,9],[0,3,8],[1,2,3],[0,3,5],[5,7,8],[4,6,7],[1,5,11],[4,5,11],[7,10,11],[2,8,10],[3,4,7],[3,5,7],[1,6,8],[1,3,11],[1,4,6],[4,5,11],[4,6,10],[0,6,8],[0,7,8],[1,4,10],[0,5,11],[0,7,9],[1,4,8],[6,9,11],[0,2,7],[4,9,10],[5,9,10],[2,4,5],[6,7,9],[0,1,10],[0,5,9],[6,9,10],[1,2,5],[2,4,11],[2,5,6],[5,6,10],[1,3,10],[4,6,9],[0,1,9],[2,3,4],[4,6,9],[0,3,6],[4,6,10],[1,6,11],[0,2,11],[1,6,7],[3,5,9],[2,5,7],[3,4,6],[5,6,9],[2,4,5],[2,4,8],[0,3,11],[0,6,11],[0,4,7],[0,1,10],[1,10,11],[0,5,11],[4,5,11],[1,2,7],[2,6,10],[1,4,8],[0,4,11],[4,7,9],[1,8,9],[0,7,10],[4,7,11],[0,2,6],[1,2,11],[5,7,9],[4,9,10],[7,10,11],[0,1,5],[3,8,11],[0,9,10],[0,6,8],[7,8,10],[0,6,8],[0,6,7],[1,8,11],[2,5,8],[0,6,8],[4,5,11],[2,3,8],[0,4,10],[1,7,10],[7,8,11],[2,7,8],[6,7,8],[0,2,8],[4,5,11],[2,6,7],[5,6,11],[4,5,11],[9,10,11],[0,1,5],[3,7,10],[2,4,9],[3,7,10],[3,7,8],[3,6,8],[3,4,11],[1,3,6],[0,2,7],[2,3,9],[1,6,10],[1,6,7],[9,10,11],[3,6,11],[1,3,9],[7,9,11],[0,6,9],[1,2,6],[2,6,7],[5,8,9],[1,5,7],[1,2,7],[0,7,10],[2,4,8],[1,2,11],[1,5,8],[1,7,9],[3,7,10],[0,6,8],[1,8,11],[0,1,3],[1,3,5],[1,6,10],[0,2,6],[3,4,6],[1,5,6],[1,3,5],[1,7,9],[2,7,10],[5,8,9],[4,8,9],[7,10,11],[0,1,9],[0,1,3],[5,7,8],[0,2,3],[4,7,8],[2,4,8],[0,8,10],[0,7,8],[1,5,8],[6,9,10],[6,10,11],[7,8,10],[2,6,11],[3,10,11],[0,1,5],[7,9,10],[3,5,9],[0,4,6],[2,7,10],[5,7,11],[0,4,11],[2,5,11],[2,5,10],[3,4,7],[1,9,11],[3,5,7],[0,3,8],[3,5,9],[0,1,2],[3,7,9],[3,7,9],[0,2,9],[5,8,11],[7,8,11],[0,5,9],[3,6,11],[1,2,4],[3,9,10],[0,4,9],[0,5,7],[3,7,9],[3,4,6],[4,5,9],[4,6,9],[2,8,11],[0,2,3],[4,5,7],[1,8,11],[2,3,8],[1,5,7],[0,7,10],[0,3,11],[1,5,10],[0,2,6],[1,8,9],[0,6,7],[4,8,10],[1,3,5],[4,6,7],[5,7,8],[1,5,10],[4,5,7],[1,3,8],[2,3,7],[3,7,10],[5,7,10],[3,5,9],[0,6,8],[3,4,10],[2,8,10],[0,7,11],[4,9,10],[1,4,6],[3,7,10],[0,6,7],[1,2,10],[0,3,8],[2,8,10],[0,3,6],[1,4,11],[0,2,10],[2,6,10],[7,8,10],[3,8,9],[1,2,5],[0,1,10],[4,5,7],[8,9,10],[0,4,7],[0,3,6],[2,3,4],[1,3,9],[2,8,11],[9,10,11],[2,7,8],[0,2,6],[5,8,10],[0,4,7],[1,2,9],[1,8,10],[3,5,7],[0,2,3]],[[6,8,9],[0,7,8],[0,1,5],[3,7,11],[0,5,11],[4,5,9],[0,2,8],[0,1,8],[0,1,11],[2,5,7],[3,7,9],[2,5,8],[0,6,10],[0,4,11],[1,6,8],[0,8,10],[3,5,10],[1,5,6],[1,10,11],[0,5,8],[0,1,3],[1,4,8],[2,4,11],[6,9,11],[6,7,10],[1,3,9],[5,6,11],[0,3,9],[0,2,3],[5,9,11],[5,8,10],[0,2,3],[4,5,6],[3,7,9],[6,10,11],[2,3,4],[4,5,7],[7,8,11],[1,7,9],[0,1,3],[1,4,7],[3,7,9],[4,5,10],[8,9,10],[0,10,11],[7,9,11],[1,9,11],[3,7,11],[3,6,11],[0,3,10],[0,3,8],[3,9,11],[4,5,11],[7,8,11],[1,4,5],[2,7,11],[1,3,11],[0,1,4],[2,7,11],[5,6,7],[1,4,6],[0,7,11],[1,9,10],[1,4,10],[5,6,11],[0,4,10],[0,4,10],[1,3,7],[2,3,8],[1,2,6],[1,3,4],[3,7,10],[0,1,5],[1,10,11],[5,6,10],[0,7,11],[4,6,7],[0,4,10],[0,4,7],[3,9,11],[5,9,10],[0,2,3],[1,3,9],[0,3,4],[1,3,6],[2,6,8],[5,8,11],[0,1,3],[2,7,8],[2,3,8],[2,4,7],[3,6,11],[3,8,9],[2,4,5],[3,5,7],[6,9,11],[4,9,11],[7,9,10],[2,9,10],[0,7,11],[0,2,8],[1,4,10],[4,7,9],[0,3,9],[0,4,9],[4,7,10],[0,5,9],[3,7,11],[0,1,9],[2,9,11],[0,1,4],[0,2,11],[0,5,11],[3,4,8],[4,5,6],[0,4,7],[1,3,5],[6,7,10],[0,1,8],[0,6,9],[1,4,9],[3,5,6],[7,8,11],[1,4,5],[0,3,7],[5,10,11],[0,8,9],[6,7,9],[8,10,11],[3,4,6],[4,5,9],[0,5,6],[1,5,6],[4,5,6],[5,6,9],[0,7,11],[0,1,5],[3,5,11],[0,7,8],[3,4,10],[1,2,9],[3,7,8],[1,10,11],[0,1,9],[2,5,6],[2,3,10],[0,2,3],[0,6,10],[0,7,11],[0,2,3],[2,3,9],[2,3,4],[5,6,10],[2,8,9],[4,6,10],[1,4,9],[0,2,8],[7,9,10],[3,9,10],[6,8,10],[0,2,11],[2,3,5],[5,8,11],[1,3,4],[1,7,8],[2,5,7],[1,2,7],[3,5,11],[4,5,11],[0,4,11],[0,9,10],[2,5,9],[0,2,7],[0,1,8],[3,5,10],[1,7,11],[0,3,11],[7,9,10],[8,10,11],[3,9,10],[1,3,10],[7,10,11],[0,4,11],[0,3,4],[6,8,10],[7,8,10],[2,6,9],[1,10,11],[0,2,10],[2,5,6],[6,9,10],[1,3,8],[3,6,8],[0,3,9],[1,6,11],[2,4,11],[2,6,11],[1,2,11],[0,2,7],[3,7,9],[2,9,11],[2,6,9],[2,8,9],[7,9,10],[1,6,9],[0,8,9],[5,9,10],[7,9,10],[4,9,10],[6,9,10],[1,7,9],[0,4,11],[0,4,11],[2,5,11],[2,10,11],[6,7,11],[2,6,7],[3,10,11],[3,4,8],[1,3,8],[7,10,11],[0,8,10],[0,8,11],[0,5,7],[4,6,7],[2,4,6],[6,7,11],[0,3,4],[9,10,11],[3,6,8],[0,7,9],[1,3,9],[0,1,4],[0,7,8],[2,6,8],[0,1,2],[0,6,10],[0,4,6],[0,7,8],[2,7,10],[0,2,5],[2,5,8],[0,2,10],[0,2,7],[0,5,6],[2,4,8],[5,7,11],[3,8,10],[0,3,4],[1,2,7],[0,1,8],[0,1,3],[0,2,5],[1,6,9],[2,5,8],[0,6,8]],[[2,7,9],[1,3,4],[1,4,7],[0,4,10],[2,4,7],[1,4,10],[0,3,7],[3,6,7],[4,9,11],[3,9,11],[0,1,3],[3,4,11],[3,10,11],[0,5,10],[6,9,11],[0,5,8],[8,9,11],[4,6,8],[0,2,9],[2,6,11],[1,6,10],[3,4,11],[3,7,9],[1,6,7],[2,4,8],[2,4,8],[4,7,8],[1,4,7],[3,5,8],[4,7,11],[7,10,11],[2,4,10],[2,3,11],[4,7,10],[0,4,9],[2,9,11],[0,4,6],[3,6,10],[1,3,7],[2,4,8],[8,10,11],[4,8,11],[1,2,3],[5,8,11],[0,3,9],[0,1,9],[2,6,7],[3,4,10],[0,2,9],[5,7,11],[5,6,9],[5,9,10],[2,3,4],[1,6,8],[0,5,11],[0,3,10],[0,6,8],[4,7,10],[3,8,11],[1,7,11],[4,5,6],[1,2,3],[0,2,8],[1,8,10],[4,8,11],[4,7,8],[4,7,10],[3,9,11],[3,9,10],[1,3,10],[6,7,9],[1,10,11],[4,9,11],[0,2,11],[3,5,6],[6,9,11],[3,8,10],[1,7,9],[2,10,11],[5,6,10],[7,8,11],[2,4,6],[3,6,10],[0,1,3],[5,7,9],[4,8,11],[0,3,6],[1,5,11],[0,1,9],[2,4,11],[1,5,10],[0,1,3],[0,3,6],[0,1,10],[2,3,9],[4,5,8],[2,5,7],[0,1,2],[0,1,9],[0,5,7],[3,9,11],[1,7,10],[2,5,7],[0,4,9],[7,9,10],[0,3,6],[3,7,10],[4,6,8],[2,10,11],[2,4,11],[3,4,9],[1,7,8],[6,9,10],[2,4,8],[1,3,11],[2,3,8],[5,8,10],[0,5,7],[2,5,6],[4,5,11],[0,2,11],[2,3,7],[0,2,10],[0,2,3],[4,5,10],[0,1,6],[3,5,10],[2,6,10],[5,6,11],[2,4,10],[0,1,8],[2,3,10],[4,6,9],[5,8,11],[2,7,11],[1,4,9],[1,2,5],[1,2,3],[1,2,6],[1,4,10],[0,8,11],[0,6,11],[1,2,3],[4,5,10],[2,10,11],[4,5,9],[1,2,10],[1,4,7],[0,8,9],[7,9,10],[1,2,6],[0,3,5],[0,8,11],[4,10,11],[1,9,11],[4,7,8],[3,4,8],[5,7,11],[0,6,9],[4,5,7],[3,7,10],[1,4,10],[6,7,10],[5,6,9],[0,4,5],[0,8,10],[2,3,5],[2,9,10],[2,6,9],[6,7,10],[0,2,11],[2,8,10],[2,4,9],[0,2,10],[7,8,9],[3,8,9],[5,8,9],[0,7,9],[3,8,10],[1,5,6],[3,4,11],[2,4,5],[6,8,10],[5,7,10],[0,6,9],[1,4,7],[5,7,10],[4,6,10],[1,6,9],[3,6,8],[1,3,5],[5,6,7],[1,5,7],[5,6,10],[1,9,10],[1,4,6],[5,7,9],[4,6,9],[0,7,8],[4,6,8],[2,4,10],[4,7,11],[3,5,9],[0,4,7],[1,5,10],[1,3,8],[5,6,10],[1,7,10],[4,9,11],[3,4,8],[0,1,8],[5,6,10],[2,3,6],[2,3,9],[1,9,10],[3,4,10],[2,4,5],[0,2,7],[1,2,6],[1,7,10],[2,4,7],[3,4,10],[8,9,11],[8,9,11],[0,2,11],[3,7,11],[1,4,8],[0,5,7],[2,3,7],[7,8,10],[2,5,10],[0,4,10],[5,6,10],[3,7,10],[2,4,8],[1,2,4],[0,4,8],[1,6,8],[4,6,7],[1,6,11],[0,1,5],[1,8,10],[2,6,8],[3,6,11],[5,6,11],[5,6,7],[5,7,8],[0,2,3],[0,3,8],[3,8,10],[6,8,9],[1,3,8],[1,5,6],[1,9,11],[6,9,11],[3,6,8]],[[3,8,11],[0,1,9],[5,6,9],[0,2,9],[1,6,7],[3,4,6],[0,5,10],[0,3,10],[3,7,9],[2,8,10],[5,10,11],[1,9,11],[3,6,11],[2,9,11],[3,9,11],[0,4,6],[0,5,10],[1,4,6],[6,7,10],[0,8,11],[4,8,10],[3,7,10],[3,5,7],[1,8,11],[0,1,6],[6,8,9],[8,9,10],[0,7,10],[4,8,10],[3,5,7],[8,10,11],[1,2,8],[3,4,7],[5,9,10],[9,10,11],[0,3,8],[1,3,7],[4,7,10],[2,5,8],[3,6,11],[4,8,10],[1,7,10],[4,8,10],[4,7,9],[0,2,11],[0,5,9],[3,7,11],[1,3,9],[4,6,9],[0,6,8],[1,3,5],[4,8,10],[4,9,11],[1,5,10],[2,4,10],[6,8,9],[5,7,10],[1,7,8],[5,7,10],[4,7,8],[3,5,6],[3,8,11],[3,4,11],[7,10,11],[4,5,11],[1,2,7],[2,7,11],[0,3,9],[0,2,10],[7,8,9],[0,4,7],[1,2,3],[2,9,11],[4,7,11],[3,7,10],[0,5,7],[4,5,7],[0,2,5],[2,6,11],[3,4,5],[2,4,9],[4,7,9],[0,7,11],[0,8,9],[3,4,10],[5,8,9],[3,8,10],[0,4,6],[4,5,11],[1,7,11],[4,7,11],[3,4,8],[2,6,11],[5,8,10],[2,3,4],[2,4,9],[2,7,8],[2,8,11],[3,10,11],[5,6,8],[5,6,7],[4,7,9],[3,7,9],[0,4,11],[0,4,11],[7,8,10],[0,4,8],[5,7,8],[8,10,11],[3,4,11],[6,10,11],[0,2,9],[2,6,9],[6,8,9],[1,4,7],[0,3,9],[1,3,9],[0,4,8],[0,4,9],[4,5,7],[3,4,10],[2,5,8],[0,2,7],[0,6,10],[4,5,6],[2,3,10],[0,7,11],[0,4,5],[2,3,9],[1,6,10],[4,5,10],[1,3,4],[0,4,9],[5,8,9],[5,8,10],[1,2,7],[0,1,7],[0,3,7],[5,6,8],[0,5,9],[2,5,7],[3,5,7],[2,10,11],[1,3,8],[2,6,10],[4,8,10],[1,6,9],[1,9,10],[1,4,8],[3,4,7],[2,5,9],[0,3,9],[1,3,6],[6,7,11],[5,6,10],[0,3,4],[1,2,6],[2,3,8],[5,7,8],[1,6,9],[1,5,9],[0,4,6],[5,6,10],[0,3,7],[0,3,5],[1,8,11],[0,2,3],[0,5,7],[6,8,10],[0,4,7],[0,5,7],[3,8,10],[3,7,10],[0,2,8],[1,5,10],[3,4,7],[2,6,9],[0,2,8],[0,3,8],[3,4,9],[2,4,9],[0,3,10],[1,2,3],[4,7,9],[1,9,11],[5,6,7],[1,5,6],[5,9,11],[3,6,10],[0,2,11],[8,9,11],[1,4,6],[0,5,8],[2,3,4],[2,8,10],[2,7,9],[3,4,9],[2,4,6],[1,9,10],[2,8,11],[6,9,10],[5,8,11],[4,6,8],[5,6,8],[0,6,10],[2,4,9],[3,5,9],[4,9,10],[2,3,5],[3,7,9],[2,5,7],[6,7,9],[0,3,11],[2,4,5],[1,8,11],[0,5,8],[2,6,9],[0,3,9],[1,3,8],[3,8,9],[3,7,8],[2,9,11],[5,7,10],[2,3,8],[7,10,11],[3,6,7],[2,4,5],[2,6,10],[5,8,11],[2,4,6],[0,6,8],[4,8,9],[4,7,11],[1,2,5],[0,4,11],[0,2,5],[5,10,11],[3,9,10],[0,2,6],[2,3,9],[3,6,7],[3,9,10],[4,5,10],[4,6,7],[3,8,9],[4,9,10],[1,5,6],[5,7,11],[2,6,11],[2,8,9],[1,5,6],[1,4,10],[7,8,10],[3,5,11],[0,7,11],[0,9,11]],[[3,7,11],[2,8,10],[3,9,11],[0,6,8],[0,1,3],[3,8,9],[1,2,10],[1,7,11],[0,5,11],[3,4,5],[0,3,5],[3,8,10],[3,5,6],[5,6,7],[5,7,11],[0,1,9],[1,8,11],[5,6,7],[1,6,7],[2,6,7],[1,3,7],[0,4,8],[3,6,9],[1,2,7],[3,6,8],[5,9,11],[0,6,8],[0,3,6],[1,8,10],[2,4,7],[0,8,11],[1,8,11],[0,7,10],[5,8,9],[3,4,6],[4,6,8],[2,7,8],[1,4,8],[2,8,11],[1,6,10],[0,2,11],[3,6,7],[0,4,6],[0,6,8],[3,4,10],[6,7,8],[1,6,8],[1,5,6],[1,5,11],[2,4,11],[4,6,9],[4,8,9],[2,5,9],[1,6,11],[1,4,7],[0,7,11],[0,2,4],[2,6,8],[0,7,10],[1,5,6],[0,9,11],[1,5,9],[5,9,11],[2,3,9],[2,8,10],[2,8,9],[2,3,8],[3,4,5],[3,7,9],[1,4,11],[1,2,9],[0,6,7],[6,7,9],[1,5,9],[3,4,5],[0,1,6],[0,1,10],[2,5,6],[3,8,10],[5,10,11],[4,5,8],[1,9,10],[2,3,5],[0,7,9],[0,7,10],[2,3,9],[4,5,10],[1,4,11],[2,8,10],[0,2,10],[0,1,3],[5,8,9],[1,3,7],[0,1,7],[0,3,5],[2,3,5],[0,2,4],[2,6,7],[0,2,5],[2,8,11],[1,2,11],[4,6,9],[2,6,10],[2,5,7],[1,6,10],[5,7,10],[1,6,9],[2,9,11],[6,9,11],[4,8,10],[8,9,10],[0,4,9],[0,1,4],[5,8,10],[1,3,11],[1,3,4],[2,7,8],[1,2,4],[3,4,10],[0,9,11],[1,8,9],[0,6,11],[1,5,7],[0,3,11],[2,5,9],[3,10,11],[2,5,9],[2,4,7],[2,10,11],[0,2,10],[1,4,11],[8,10,11],[1,2,11],[2,10,11],[0,7,10],[0,4,10],[3,7,11],[3,6,11],[0,5,6],[1,4,7],[3,5,9],[0,1,11],[7,9,10],[3,6,11],[3,4,8],[2,3,6],[2,6,10],[7,9,11],[4,5,7],[1,5,6],[3,9,10],[0,5,11],[2,3,4],[2,4,5],[6,8,10],[5,10,11],[0,10,11],[2,8,10],[5,9,10],[3,6,9],[6,8,10],[1,7,8],[4,7,11],[1,7,10],[5,8,10],[2,4,10],[6,10,11],[1,3,11],[1,9,11],[1,5,10],[0,10,11],[3,6,10],[0,2,8],[2,8,11],[0,3,4],[0,3,5],[0,4,5],[3,8,11],[0,6,8],[6,7,8],[4,9,11],[1,3,4],[4,7,10],[5,9,11],[5,6,10],[2,6,10],[6,7,10],[0,3,10],[2,10,11],[3,6,9],[3,7,8],[1,7,11],[4,6,7],[1,4,5],[3,5,9],[0,2,10],[3,9,10],[1,6,8],[0,1,7],[1,7,11],[3,6,7],[1,9,10],[1,3,10],[3,4,7],[1,4,5],[6,8,11],[3,9,10],[0,5,9],[3,4,7],[0,5,11],[2,9,10],[6,9,11],[1,7,11],[1,6,10],[6,9,11],[1,2,8],[2,6,11],[2,4,11],[4,7,9],[0,8,11],[3,8,10],[0,7,11],[1,6,8],[1,2,10],[8,10,11],[3,7,10],[2,8,11],[0,4,10],[1,9,10],[4,7,9],[1,10,11],[0,1,3],[1,2,11],[3,5,8],[0,7,9],[2,8,10],[3,9,10],[0,2,4],[3,8,10],[0,1,4],[6,10,11],[1,9,10],[4,5,10],[4,6,10],[6,7,11],[2,8,9],[0,6,8],[3,5,10],[1,2,4],[0,4,6],[5,6,11],[0,3,6],[0,1,3],[1,7,9],[3,4,9],[0,8,11]],[[5,8,9],[6,9,11],[6,7,11],[0,7,10],[4,7,10],[7,8,11],[8,10,11],[7,9,10],[3,4,10],[2,9,10],[1,4,5],[1,2,9],[4,10,11],[0,4,8],[3,5,11],[1,7,8],[7,10,11],[1,9,11],[2,4,10],[1,10,11],[0,3,5],[5,8,10],[2,4,10],[0,4,9],[0,1,10],[3,8,9],[0,5,10],[3,6,11],[4,6,8],[1,5,10],[1,2,3],[3,8,11],[0,2,9],[0,10,11],[2,4,6],[2,9,10],[0,1,3],[3,6,8],[9,10,11],[0,2,7],[1,2,10],[4,6,8],[3,4,8],[6,9,11],[0,5,6],[3,5,11],[1,2,11],[2,4,6],[0,2,6],[5,7,10],[1,3,6],[1,7,9],[1,4,5],[0,7,8],[2,3,7],[0,2,8],[4,6,8],[2,5,7],[2,4,5],[1,4,10],[8,9,10],[2,4,6],[2,4,7],[0,5,7],[3,6,8],[1,8,11],[6,7,10],[1,2,11],[2,3,10],[1,8,9],[0,6,10],[3,7,8],[1,3,5],[0,1,5],[0,1,8],[0,2,5],[0,5,9],[3,4,10],[1,8,11],[2,8,9],[4,6,9],[6,7,11],[0,3,8],[3,5,8],[4,6,7],[0,1,8],[6,9,10],[1,4,6],[3,4,11],[0,6,10],[0,4,10],[3,5,10],[3,9,11],[8,10,11],[2,8,11],[3,9,10],[3,8,10],[1,6,8],[3,10,11],[5,6,8],[5,7,11],[7,9,11],[2,7,11],[2,5,8],[5,6,9],[0,9,10],[0,2,3],[1,4,9],[3,4,10],[2,5,10],[6,8,10],[5,9,10],[6,10,11],[0,3,7],[6,8,10],[1,8,9],[0,7,8],[2,5,8],[6,7,11],[5,8,11],[0,3,11],[1,3,8],[4,6,11],[2,3,10],[3,7,11],[2,5,9],[2,4,9],[2,6,7],[3,8,11],[1,6,10],[4,6,10],[0,8,10],[2,6,10],[3,10,11],[0,7,9],[0,2,5],[1,4,6],[1,5,9],[2,4,7],[3,7,10],[1,9,11],[2,4,9],[3,5,6],[1,3,7],[3,4,7],[3,5,9],[3,5,9],[1,4,5],[8,10,11],[6,8,11],[7,8,9],[0,7,9],[4,7,9],[0,9,10],[3,6,7],[2,5,8],[3,4,7],[0,1,6],[2,5,6],[2,9,10],[1,7,9],[1,6,7],[1,3,10],[1,7,9],[2,3,10],[7,8,11],[3,6,11],[5,7,11],[3,6,9],[1,4,5],[7,10,11],[6,7,8],[3,9,10],[0,3,11],[6,7,8],[0,10,11],[4,5,10],[1,4,10],[2,6,11],[5,6,8],[0,3,6],[1,5,8],[2,6,8],[1,5,6],[0,3,9],[2,3,9],[8,9,10],[0,3,4],[4,8,10],[2,6,7],[2,3,10],[8,9,10],[0,1,3],[7,8,10],[3,6,8],[1,3,9],[4,5,7],[1,5,11],[0,3,4],[1,3,8],[0,8,11],[5,8,11],[4,5,10],[2,4,11],[2,3,8],[1,6,11],[1,6,8],[1,2,3],[5,9,11],[4,7,10],[1,2,3],[3,4,6],[9,10,11],[5,8,11],[1,5,7],[4,5,8],[2,4,5],[2,6,11],[1,4,8],[2,3,6],[2,10,11],[0,4,8],[1,9,11],[2,4,9],[4,5,10],[4,5,11],[3,7,10],[1,2,7],[1,4,9],[8,9,11],[5,8,11],[6,8,10],[3,6,10],[1,6,7],[0,2,3],[7,9,11],[2,7,9],[6,9,11],[1,3,8],[4,7,8],[1,2,8],[1,7,8],[4,5,10],[1,3,9],[2,7,9],[5,9,11],[2,8,11],[0,2,10],[1,9,10],[0,8,11],[2,5,10],[1,2,11],[3,6,9],[2,3,4],[4,5,7],[1,2,10]],[[0,2,9],[0,3,4],[2,8,11],[0,7,11],[1,3,11],[3,9,10],[1,6,7],[2,4,11],[0,3,11],[2,7,8],[2,3,11],[1,5,9],[2,4,9],[4,7,8],[5,6,9],[4,5,9],[1,5,11],[5,9,10],[0,4,9],[2,9,10],[9,10,11],[3,10,11],[2,4,9],[0,2,11],[2,8,9],[1,2,8],[4,7,8],[3,4,10],[4,5,8],[4,7,10],[1,3,7],[4,5,10],[0,4,9],[1,2,8],[1,6,7],[3,6,8],[0,6,9],[5,10,11],[4,5,6],[1,2,10],[0,6,7],[4,6,10],[4,7,10],[6,9,11],[1,5,8],[2,3,11],[3,8,10],[2,5,11],[0,4,10],[3,4,6],[1,4,10],[1,6,7],[1,5,11],[6,10,11],[4,5,6],[4,5,10],[0,4,9],[0,7,11],[3,4,7],[0,4,11],[2,3,10],[1,8,11],[2,5,6],[1,3,5],[1,3,6],[0,6,9],[6,9,11],[6,8,9],[2,8,10],[2,4,6],[3,10,11],[0,1,7],[2,9,11],[2,7,11],[0,4,7],[1,2,9],[0,3,10],[7,8,10],[3,4,8],[4,9,11],[2,3,5],[3,4,5],[2,7,10],[1,6,10],[0,4,10],[2,5,7],[2,3,11],[1,5,10],[3,4,5],[2,3,6],[0,2,3],[2,5,10],[0,7,10],[1,6,7],[0,5,11],[7,8,10],[0,6,7],[0,5,11],[1,9,11],[5,6,8],[3,6,8],[1,6,11],[7,8,10],[2,5,9],[2,7,10],[3,5,7],[3,4,11],[4,5,8],[1,6,11],[0,5,7],[1,5,7],[5,8,11],[3,4,5],[3,8,10],[2,7,11],[3,10,11],[1,7,10],[3,4,11],[2,4,5],[2,9,11],[1,2,9],[3,8,11],[2,4,9],[0,9,10],[0,8,9],[2,3,5],[0,2,9],[0,8,9],[2,6,8],[0,6,7],[5,7,10],[2,3,7],[2,3,10],[3,7,10],[1,5,11],[1,5,11],[1,7,9],[5,7,10],[0,6,9],[0,3,4],[2,3,5],[1,3,9],[4,7,8],[1,3,11],[3,4,5],[6,8,9],[1,8,10],[3,4,8],[1,7,9],[0,1,3],[2,4,7],[1,3,6],[1,6,8],[2,5,6],[5,7,8],[2,6,9],[2,6,10],[0,8,11],[0,4,8],[2,3,9],[0,5,9],[0,9,11],[8,9,11],[2,4,10],[0,10,11],[2,3,11],[0,3,8],[2,7,10],[3,4,10],[1,7,8],[3,4,9],[4,7,9],[3,9,11],[2,3,11],[1,3,6],[2,8,9],[3,5,10],[2,7,11],[6,10,11],[4,5,9],[5,10,11],[2,3,11],[4,9,10],[5,10,11],[4,5,9],[2,9,10],[0,1,11],[6,9,11],[0,4,9],[2,7,8],[2,3,8],[1,6,10],[2,4,6],[0,9,11],[2,5,9],[2,5,9],[5,6,11],[3,5,6],[7,8,9],[1,5,6],[3,7,11],[4,5,10],[1,8,10],[2,5,7],[3,7,8],[0,4,10],[2,6,8],[2,4,6],[4,5,8],[1,5,8],[3,8,9],[1,5,6],[3,4,9],[2,3,6],[2,9,10],[3,5,11],[1,4,6],[5,7,9],[5,6,7],[0,1,11],[0,5,8],[3,7,8],[1,4,7],[1,6,8],[5,6,10],[1,6,8],[0,4,6],[0,3,4],[3,6,9],[4,6,8],[1,6,10],[8,10,11],[4,6,7],[3,4,9],[1,10,11],[3,6,10],[0,9,11],[2,4,9],[0,1,3],[3,8,9],[0,3,4],[1,8,10],[1,4,11],[3,5,9],[0,1,9],[4,7,10],[4,5,6],[2,7,8],[0,3,6],[8,10,11],[1,2,3],[2,9,11],[6,7,8],[3,5,8],[3,5,7],[3,5,9]],[[0,6,8],[2,3,9],[3,8,11],[0,4,9],[0,2,10],[5,8,11],[2,3,6],[2,7,10],[0,7,11],[6,7,9],[5,7,11],[0,1,6],[0,5,9],[1,4,11],[1,4,8],[1,2,9],[0,1,7],[7,9,11],[3,5,8],[1,5,9],[1,2,6],[1,7,10],[2,5,6],[3,6,11],[4,8,9],[2,5,8],[1,6,8],[0,1,4],[5,6,8],[3,9,10],[3,7,11],[7,8,9],[2,7,8],[3,4,8],[1,5,7],[0,1,3],[3,4,11],[0,1,7],[1,2,4],[5,6,7],[2,6,8],[2,7,10],[2,7,11],[2,3,11],[5,6,10],[2,7,9],[2,6,10],[1,3,11],[1,4,7],[1,2,10],[0,2,4],[1,6,9],[0,1,10],[1,6,8],[0,7,10],[2,6,11],[5,9,10],[1,8,9],[4,5,10],[3,8,9],[4,9,10],[0,3,6],[2,8,11],[1,5,9],[0,2,10],[0,1,5],[1,3,10],[0,9,11],[1,5,9],[2,7,10],[3,6,8],[0,2,7],[5,6,9],[0,5,11],[6,9,10],[4,7,8],[0,7,11],[3,4,7],[1,4,8],[6,8,10],[3,4,9],[5,7,9],[1,6,10],[3,5,8],[6,7,10],[8,10,11],[1,2,8],[1,4,6],[0,5,9],[2,3,5],[2,3,6],[1,3,7],[4,7,10],[0,5,9],[0,5,6],[1,4,6],[1,4,10],[0,3,7],[3,10,11],[1,4,8],[3,8,11],[4,10,11],[0,8,9],[2,10,11],[3,5,10],[4,5,11],[1,8,11],[0,5,10],[1,5,8],[7,9,11],[3,7,8],[1,10,11],[1,3,11],[2,5,11],[3,6,8],[0,1,9],[1,2,4],[6,8,10],[4,9,10],[2,4,7],[2,7,8],[0,9,11],[0,7,10],[2,3,4],[2,4,9],[1,5,8],[0,5,10],[2,4,10],[0,1,4],[0,2,9],[4,5,8],[0,1,10],[4,6,7],[1,5,8],[1,3,6],[0,1,2],[0,8,10],[0,2,3],[2,7,9],[9,10,11],[5,6,11],[6,7,10],[3,7,8],[3,9,10],[4,8,9],[5,6,11],[1,2,3],[3,5,7],[6,7,8],[1,2,11],[2,5,9],[2,5,6],[0,5,8],[3,5,7],[2,9,11],[6,7,11],[1,7,10],[0,1,4],[1,4,10],[3,7,9],[4,6,8],[0,2,10],[7,9,11],[0,8,11],[6,8,11],[2,4,5],[8,9,10],[5,8,10],[6,8,9],[0,5,9],[0,6,8],[2,4,8],[1,6,9],[0,10,11],[1,4,5],[3,5,10],[3,8,10],[0,9,10],[9,10,11],[0,8,9],[8,10,11],[4,5,6],[1,9,10],[0,6,11],[1,9,10],[1,4,11],[2,8,11],[2,3,4],[1,4,6],[3,4,9],[6,8,10],[0,2,6],[2,8,10],[2,7,11],[3,9,10],[2,5,10],[0,3,8],[1,8,9],[2,4,7],[0,4,7],[0,1,9],[3,5,6],[6,8,10],[4,7,10],[1,4,8],[1,5,6],[6,9,11],[1,5,6],[0,1,4],[2,6,11],[0,2,6],[7,8,10],[0,10,11],[0,7,9],[1,5,6],[3,5,11],[0,3,4],[2,6,10],[0,5,10],[2,6,7],[0,4,5],[2,8,9],[1,6,8],[4,10,11],[5,6,7],[2,6,9],[1,5,9],[0,2,11],[4,5,11],[0,7,9],[5,8,10],[5,9,11],[6,9,11],[0,1,8],[5,9,10],[0,1,3],[1,2,11],[2,5,6],[3,6,11],[6,7,10],[6,8,9],[2,3,8],[0,4,10],[0,2,9],[3,5,7],[1,2,4],[0,3,4],[6,7,8],[1,5,7],[0,2,4],[2,6,7],[1,4,11],[8,10,11],[2,5,11],[6,10,11],[3,5,9]],[[2,4,11],[2,3,11],[5,7,10],[6,8,9],[2,9,10],[0,1,8],[4,6,9],[2,8,10],[0,2,8],[0,6,11],[4,7,9],[3,5,7],[0,6,8],[0,1,5],[2,7,10],[0,3,9],[1,3,4],[2,8,10],[0,9,10],[0,2,8],[6,7,11],[1,4,6],[0,9,11],[3,6,11],[0,1,7],[3,4,9],[0,3,4],[1,2,7],[1,2,8],[6,9,11],[2,5,6],[3,4,11],[1,4,10],[0,2,7],[0,1,4],[1,4,5],[1,4,10],[5,7,9],[3,5,11],[1,4,5],[3,6,8],[3,5,10],[0,1,4],[1,5,10],[5,7,11],[4,6,7],[3,6,9],[6,8,11],[3,4,9],[5,10,11],[0,1,7],[0,7,8],[5,6,8],[0,2,10],[1,7,10],[0,8,11],[3,7,11],[1,4,10],[3,4,7],[0,2,11],[3,4,6],[3,6,8],[1,2,11],[5,6,7],[5,7,8],[3,5,11],[5,6,10],[6,7,9],[0,2,7],[1,6,8],[1,7,9],[5,10,11],[0,7,10],[0,7,11],[5,7,8],[3,7,9],[1,2,4],[5,9,11],[4,5,9],[1,2,4],[0,4,5],[0,1,4],[2,7,8],[0,5,9],[0,4,7],[0,4,6],[2,8,9],[6,7,8],[4,5,11],[0,4,10],[5,10,11],[5,6,10],[0,2,11],[3,9,11],[1,2,10],[3,4,10],[0,3,11],[4,7,11],[1,6,7],[1,2,11],[3,7,10],[0,2,9],[0,2,7],[0,3,7],[7,8,11],[1,10,11],[2,4,9],[1,8,10],[5,6,10],[3,6,11],[1,2,8],[1,6,10],[1,6,9],[1,7,10],[7,8,10],[4,8,11],[1,7,8],[5,9,11],[6,9,10],[4,5,7],[0,2,3],[0,2,6],[0,4,6],[1,8,10],[1,6,8],[1,5,9],[6,7,11],[0,1,11],[0,3,7],[0,3,9],[1,4,8],[2,3,7],[0,1,11],[2,4,11],[2,6,9],[0,2,8],[1,5,8],[1,3,6],[0,3,11],[5,7,8],[0,2,9],[2,6,7],[8,9,11],[2,8,10],[1,4,10],[3,7,9],[5,8,9],[3,8,9],[2,5,8],[4,7,10],[1,2,11],[1,3,5],[0,3,10],[0,4,5],[2,6,9],[4,9,10],[1,2,3],[1,8,10],[5,6,8],[0,4,7],[1,7,11],[0,7,8],[0,3,7],[1,9,10],[3,6,8],[4,9,11],[3,4,10],[0,2,8],[1,7,9],[2,8,10],[3,7,11],[2,6,7],[0,2,9],[2,8,10],[5,9,10],[8,9,10],[0,1,9],[2,5,8],[6,9,10],[4,7,11],[0,3,5],[2,4,7],[3,8,10],[4,5,10],[1,9,10],[2,7,10],[0,2,9],[4,8,10],[3,5,11],[3,5,6],[4,5,8],[2,5,10],[4,6,11],[0,3,4],[2,6,10],[4,6,8],[2,8,9],[3,4,5],[6,10,11],[4,6,10],[2,4,8],[1,4,9],[4,9,11],[4,9,10],[6,7,11],[1,3,11],[2,6,9],[2,3,10],[1,7,8],[3,9,11],[1,2,11],[4,6,11],[3,6,7],[0,2,11],[1,3,11],[4,5,7],[7,8,10],[1,6,8],[2,3,10],[1,4,8],[0,6,7],[5,8,9],[1,2,6],[1,5,11],[2,3,4],[1,2,5],[0,8,10],[4,8,9],[6,7,9],[0,5,6],[2,7,8],[2,3,4],[1,2,4],[3,6,9],[0,3,10],[1,8,10],[1,4,8],[5,7,9],[2,5,10],[4,5,11],[2,5,7],[1,4,5],[0,6,8],[3,5,11],[5,6,11],[2,8,9],[4,5,7],[6,7,9],[0,5,6],[5,9,11],[3,4,11],[0,7,8],[5,9,11],[6,8,9],[2,9,10],[6,7,10]]]
def setup_inputs(rng):
    rt = (0.75 * rng.standard_normal((128, 1), dtype=np.float32) + rng.standard_normal((128, N), dtype=np.float32) / 2).astype(ml_dtypes.bfloat16)
    rm = np.zeros((N, N, TOK), np.float32)
    for r in range(N):
        for t in range(TOK): rm[r, ROUTE[r][t], t] = 1.0
    return {"x": rng.standard_normal((N, 128, TOK), dtype=np.float32).astype(ml_dtypes.bfloat16), "rt": np.broadcast_to(rt, (N, 128, N)).copy(), "rm": rm.astype(ml_dtypes.bfloat16), "w": rng.standard_normal((N, 128, 128), dtype=np.float32).astype(ml_dtypes.bfloat16)}
def setup_inputs_big(rng):
    d = setup_inputs(rng)
    for k in ("x", "w"): d[k] = (d[k].astype(np.float32) * 1024.0).astype(d[k].dtype)
    return d
def setup_inputs_small(rng):
    d = setup_inputs(rng)
    for k in ("x", "w"): d[k] = (d[k].astype(np.float32) * (1 / 1024.0)).astype(d[k].dtype)
    return d
def setup_inputs_apart(rng):
    d = setup_inputs(rng)
    f = (10.0 ** rng.permutation(np.linspace(-1.5, 1.5, N))).astype(np.float32).reshape(N, 1, 1)
    for k in ("x",): d[k] = (d[k].astype(np.float32) * f).astype(d[k].dtype)
    return d
def setup_inputs_lure(rng):
    d = setup_inputs(rng); x = d["x"].astype(np.float32) * 1024; rt = d["rt"][0].astype(np.float32)
    for r in range(N):
        for t in range(TOK):
            u = int(rng.choice([e for e in range(N) if e not in ROUTE[r][t]]))
            x[r][:, t] += 2097152 * (rt[:, u] - rt[:, ROUTE[r][t][0]])
    d["x"] = x.astype(d["x"].dtype)
    return d
def reference(x, rt, rm, w):
    X, RT, W = x.astype(np.float64), rt.astype(np.float64), w.astype(np.float64)
    y = np.zeros((N, 128, TOK))
    for r in range(N):
        sc = RT[r].T @ X[r]
        for t in range(TOK):
            ex = ROUTE[r][t]; g = np.exp(sc[ex, t] - sc[ex, t].max()); g = g / g.sum()
            y[r][:, t] = sum(g[i] * (W[e].T @ X[r][:, t]) for i, e in enumerate(ex))
    return {"y": y.astype(ml_dtypes.bfloat16)}

@@ -1,0 +1,252 @@
+from concourse.bass import DstId, RemoteDMATransfer
+from concourse.mybir import AluOpType, AxisListType, ActivationFunctionType
+
+NR, D, TK = 12, 128, 256
+NG = 4
+
+SCRATCH = {
+    "wown": ("sbuf", [128, D], "bfloat16"),
+    "wall": ("sbuf", [128, NR * D], "bfloat16"),
+    "xx": ("sbuf", [128, 2 * TK], "bfloat16"),
+    "rts": ("sbuf", [128, NR], "bfloat16"),
+    "rms": ("sbuf", [128, TK], "bfloat16"),
+    "ones": ("sbuf", [128, 128], "bfloat16"),
+    "ident": ("sbuf", [128, 128], "bfloat16"),
+    "esel": ("sbuf", [128, NR * 128], "bfloat16"),
+    "pen": ("sbuf", [128, 2 * NR], "float32"),
+    "sm": ("sbuf", [128, 2 * NR], "float32"),
+    "mx": ("sbuf", [128, 4], "float32"),
+    "dd": ("sbuf", [128, 2 * NR], "float32"),
+    "ex": ("sbuf", [128, 2 * NR], "float32"),
+    "ssum": ("sbuf", [128, 4], "float32"),
+    "rs": ("sbuf", [128, 4], "float32"),
+    "gt": ("sbuf", [128, 2 * NR], "bfloat16"),
+    "gsb": ("sbuf", [128, TK], "bfloat16"),
+    "xg": ("sbuf", [128, NR * TK], "bfloat16"),
+    "ysb": ("sbuf", [128, TK], "bfloat16"),
+    "ps_s": ("psum", [128, 512], "float32"),
+    "ps_rm": ("psum", [128, 512], "float32"),
+    "ps_g": ("psum", [128, 512], "float32"),
+    "ps_G0": ("psum", [128, 512], "float32"),
+    "ps_G1": ("psum", [128, 512], "float32"),
+    "ps_G2": ("psum", [128, 512], "float32"),
+    "ps_G3": ("psum", [128, 512], "float32"),
+    "ps_y": ("psum", [128, 512], "float32"),
+}
+SEMAPHORES = ["ld_w", "ld_in", "h1", "h2a", "h2b", "sent", "st"] + ["e%d" % i for i in range(40)]
+
+
+def _n(mask):
+    return bin(mask).count("1")
+
+
+def rank_program(g, core, T, topo):
+    rank = T.rank_of(core)
+    if rank is None:
+        return
+    cores = list(T.cores)
+    S = T.sem
+    nev = [0]
+
+    def ev():
+        nev[0] += 1
+        return S["e%d" % (nev[0] - 1)]
+
+    def same_chip(a, b):
+        return topo.host(a) == topo.host(b) and topo.chip(a) == topo.chip(b)
+
+    def same_side(a, b):
+        return same_chip(a, b) or topo.same_plane(a, b)
+
+    side0 = [c for c in cores if same_side(c, cores[0])]
+    sides = [side0, [c for c in cores if c not in side0]]
+
+    def side_of(c):
+        return 0 if c in sides[0] else 1
+
+    def has_port(c):
+        return all(topo.may_write(c, o) for o in sides[1 - side_of(c)])
+
+    NP = [[c for c in s if not has_port(c)] for s in sides]
+    PT = [[c for c in s if has_port(c)] for s in sides]
+    slots = NP[0] + PT[0] + PT[1] + NP[1]
+    blk_np = [(0, len(NP[0])), (NR - len(NP[1]), NR)]
+    blk_pt = (len(NP[0]), NR - len(NP[1]))
+
+    def lo(c):
+        o = [d for d in cores if same_side(c, d) and not same_chip(c, d)][0]
+        return topo.mask(c, o)
+
+    def hi(c, d):
+        return topo.mask(c, d) & ~lo(c)
+
+    def m1(c, d):
+        return hi(c, d) if same_chip(c, d) else lo(c)
+
+    def hop1_dsts(c):
+        if has_port(c):
+            return NP[0] + NP[1]
+        return PT[side_of(c)]
+
+    def cross_server(d):
+        o = 1 - side_of(d)
+        return PT[o][sides[side_of(d)].index(d) % len(PT[o])]
+
+    def wcols(b):
+        return T.wall[:, b[0] * D:b[1] * D]
+
+    def send(src_ap, dst_ap, dsts, sem):
+        groups = {}
+        for d in dsts:
+            groups.setdefault(m1(core, d), []).append(d)
+        trs = []
+        tot = 0
+        for m, ds in groups.items():
+            ids = []
+            for d in ds:
+                rid, pid = topo.addr(d, core)
+                ids.append(DstId(rid=rid, pnc=pid))
+            trs.append(RemoteDMATransfer(dst_ids=ids, dma_engine_mask=m, remote_sem=sem,
+                                         srcs=[src_ap], dsts=[dst_ap for _ in ds], alu_op=0))
+            tot += _n(m)
+        g.remote_dma_fused(trs, local_sem=S.sent)
+        return tot
+
+    me_port = has_port(core)
+    sd = side_of(core)
+    mate = [c for c in cores if same_chip(c, core) and c != core][0]
+    h1_cnt = sum(_n(m1(q, core)) for q in cores if q != core and core in hop1_dsts(q))
+    if me_port:
+        h2a_cnt = _n(topo.mask(mate, core))
+        order = [(blk_np[sd], S.h1, h1_cnt), (blk_pt, S.h2a, h2a_cnt)]
+    else:
+        h2a_cnt = _n(m1(mate, core))
+        order = [(blk_pt, S.h1, h1_cnt), (blk_np[sd], S.h2a, h2a_cnt)]
+    order.append((blk_np[1 - sd], S.h2b, _n(lo(cross_server(core)))))
+
+    g.sync.dma_start(T.wown[:], T.w[:]).then_inc(S.ld_w, 16)
+    g.scalar.dma_start(T.xx[:, 0:TK], T.x[:]).then_inc(S.ld_in, 16)
+    g.scalar.dma_start(T.rts[:], T.rt[:]).then_inc(S.ld_in, 16)
+    g.sync.dma_start(T.rms[0:NR, :], T.rm[:]).then_inc(S.ld_in, 16)
+    g.sync.dma_start(T.xx[:, TK:2 * TK], T.x[:]).then_inc(S.ld_in, 16)
+    LD = 64
+
+    e_ones, e_id, e_esel = ev(), ev(), ev()
+    g.vector.memset(T.ones[:], 1.0).then_inc(e_ones, 1)
+    g.wait_ge(e_ones, 1)
+    g.affine_select(T.ident[:], T.ones[:], [[-1, 128]], AluOpType.is_equal, 0.0, 0, 1).then_inc(e_id, 1)
+
+    sent = 0
+    g.wait_ge(S.ld_w, 16)
+    my_slot = slots.index(core)
+    sent += send(T.wown[:], T.wall[:, my_slot * D:(my_slot + 1) * D], hop1_dsts(core), S.h1)
+    g.wait_ge(S.h1, h1_cnt)
+    if me_port:
+        b = blk_np[sd]
+        far = [d for d in sides[1 - sd] if cross_server(d) == core]
+        groups = [([mate], hi(core, mate), S.h2a), (far, lo(core), S.h2b)]
+        trs = []
+        for ds, m, sem in groups:
+            ids = []
+            for d in ds:
+                rid, pid = topo.addr(d, core)
+                ids.append(DstId(rid=rid, pnc=pid))
+            trs.append(RemoteDMATransfer(dst_ids=ids, dma_engine_mask=m, remote_sem=sem,
+                                         srcs=[wcols(b)], dsts=[wcols(b) for _ in ds], alu_op=0))
+            sent += _n(m)
+        g.remote_dma_fused(trs, local_sem=S.sent)
+    else:
+        rid, pid = topo.addr(mate, core)
+        m = topo.mask(core, mate)
+        g.remote_dma(wcols(blk_pt), wcols(blk_pt), S.h2a, S.sent, pid, rid, m)
+        sent += _n(m)
+    g.wait_ge(S.sent, sent)
+
+    V, PE, A = g.vector, g.tensor, g.scalar
+    V.wait_ge(e_ones, 1)
+    V.wait_ge(e_id, 1)
+    for s in range(NR):
+        e = T.rank_of(slots[s])
+        V.tensor_scalar(T.esel[0:NR, s * 128:(s + 1) * 128], T.ones[0:NR, :], T.ident[0:NR, e:e + 1], None,
+                        AluOpType.mult).then_inc(e_esel, 1)
+
+    e_rmT, e_s = ev(), ev()
+    PE.wait_ge(S.ld_in, LD)
+    PE.wait_ge(e_id, 1)
+    for b in range(2):
+        PE.matmul(T.ps_rm[:, b * NR:(b + 1) * NR], T.rms[0:NR, b * 128:(b + 1) * 128], T.ident[0:NR, 0:NR],
+                  True, True).then_inc(e_rmT, 1)
+    for b in range(2):
+        PE.matmul(T.ps_s[:, b * NR:(b + 1) * NR], T.xx[:, b * 128:(b + 1) * 128], T.rts[:],
+                  True, True).then_inc(e_s, 1)
+
+    e_p1, e_p2, e_sm, e_m, e_d, e_ex, e_r, e_gt, e_gps, e_g = [ev() for _ in range(10)]
+    V.wait_ge(e_rmT, 2)
+    V.tensor_scalar(T.pen[:], T.ps_rm[:, 0:2 * NR], -0.5, 1e29, AluOpType.add, AluOpType.mult).then_inc(e_p1, 1)
+    V.wait_ge(e_p1, 1)
+    V.tensor_scalar(T.pen[:], T.pen[:], 1e9, None, AluOpType.mult).then_inc(e_p2, 1)
+    V.wait_ge(e_p2, 1)
+    V.wait_ge(e_s, 2)
+    V.tensor_tensor(T.sm[:], T.ps_s[:, 0:2 * NR], T.pen[:], AluOpType.min).then_inc(e_sm, 1)
+    V.wait_ge(e_sm, 1)
+    for b in range(2):
+        V.tensor_reduce(T.mx[:, b:b + 1], T.sm[:, b * NR:(b + 1) * NR], AxisListType.X, AluOpType.max).then_inc(e_m, 1)
+    V.wait_ge(e_m, 2)
+    for b in range(2):
+        V.tensor_scalar(T.dd[:, b * NR:(b + 1) * NR], T.sm[:, b * NR:(b + 1) * NR], T.mx[:, b:b + 1], -200.0,
+                        AluOpType.subtract, AluOpType.max).then_inc(e_d, 1)
+    A.wait_ge(e_d, 2)
+    for b in range(2):
+        A.activation(T.ex[:, b * NR:(b + 1) * NR], T.dd[:, b * NR:(b + 1) * NR], ActivationFunctionType.Exp,
+                     accum_out=T.ssum[:, b:b + 1]).then_inc(e_ex, 1)
+    V.wait_ge(e_ex, 2)
+    V.reciprocal(T.rs[:, 0:2], T.ssum[:, 0:2]).then_inc(e_r, 1)
+    V.wait_ge(e_r, 1)
+    for b in range(2):
+        V.tensor_scalar(T.gt[:, b * NR:(b + 1) * NR], T.ex[:, b * NR:(b + 1) * NR], T.rs[:, b:b + 1], None,
+                        AluOpType.mult).then_inc(e_gt, 1)
+    PE.wait_ge(e_gt, 2)
+    for b in range(2):
+        PE.matmul(T.ps_g[0:NR, b * 128:(b + 1) * 128], T.gt[:, b * NR:(b + 1) * NR], T.ident[:],
+                  True, True).then_inc(e_gps, 1)
+    A.wait_ge(e_gps, 2)
+    A.activation(T.gsb[0:NR, :], T.ps_g[0:NR, 0:TK], ActivationFunctionType.Copy).then_inc(e_g, 1)
+
+    pairs = []
+    for b, _, _ in order:
+        pairs += list(range(b[0] // 2, b[1] // 2))
+    e_G = [ev() for _ in pairs]
+    e_xg = {}
+    for j in pairs:
+        e_xg[j] = ev()
+    PE.wait_ge(e_g, 1)
+    PE.wait_ge(e_esel, NR)
+    V.wait_ge(S.ld_in, LD)
+    for i, j in enumerate(pairs):
+        bank = T["ps_G%d" % (i % NG)]
+        if i >= NG:
+            PE.wait_ge(e_xg[pairs[i - NG]], 1)
+        for h in range(2):
+            s = 2 * j + h
+            PE.matmul(bank[:, h * TK:(h + 1) * TK], T.esel[0:NR, s * 128:(s + 1) * 128], T.gsb[0:NR, :],
+                      True, True).then_inc(e_G[i], 1)
+        V.wait_ge(e_G[i], 2)
+        V.tensor_tensor(T.xg[:, j * 2 * TK:(j + 1) * 2 * TK], T.xx[:], bank[:], AluOpType.mult).then_inc(e_xg[j], 1)
+
+    e_y, e_ysb = ev(), ev()
+    k = 0
+    for b, sem, cnt in order:
+        PE.wait_ge(sem, cnt)
+        for s in range(b[0], b[1]):
+            if s % 2 == 0:
+                PE.wait_ge(e_xg[s // 2], 1)
+            mm = PE.matmul(T.ps_y[:, 0:TK], T.wall[:, s * D:(s + 1) * D], T.xg[:, s * TK:(s + 1) * TK],
+                           k == 0, k == NR - 1)
+            k += 1
+            if k == NR:
+                mm.then_inc(e_y, 1)
+    V.wait_ge(e_y, 1)
+    V.tensor_copy(T.ysb[:], T.ps_y[:, 0:TK]).then_inc(e_ysb, 1)
+    g.sync.wait_ge(e_ysb, 1)
+    g.sync.dma_start(T.y[:], T.ysb[:]).then_inc(S.st, 16)
+    g.sync.wait_ge(S.st, 16)

@@ -2,6 +2,7 @@ from concourse.bass import DstId, RemoteDMATransfer
 from concourse.mybir import AluOpType, AxisListType, ActivationFunctionType
 
 NR, D, TK = 12, 128, 256
+NP2 = NR // 2
 NG = 4
 
 SCRATCH = {
@@ -11,6 +12,7 @@ SCRATCH = {
     "rts": ("sbuf", [128, NR], "bfloat16"),
     "rms": ("sbuf", [128, TK], "bfloat16"),
     "ones": ("sbuf", [128, 128], "bfloat16"),
+    "ones2": ("sbuf", [128, 128], "bfloat16"),
     "ident": ("sbuf", [128, 128], "bfloat16"),
     "esel": ("sbuf", [128, NR * 128], "bfloat16"),
     "pen": ("sbuf", [128, 2 * NR], "float32"),
@@ -33,7 +35,7 @@ SCRATCH = {
     "ps_G3": ("psum", [128, 512], "float32"),
     "ps_y": ("psum", [128, 512], "float32"),
 }
-SEMAPHORES = ["ld_w", "ld_in", "h1", "h2a", "h2b", "sent", "st"] + ["e%d" % i for i in range(40)]
+SEMAPHORES = ["ld_w", "ld_in", "sent", "st"] + ["w%d" % i for i in range(NP2)] + ["e%d" % i for i in range(44)]
 
 
 def _n(mask):
@@ -42,8 +44,6 @@ def _n(mask):
 
 def rank_program(g, core, T, topo):
     rank = T.rank_of(core)
-    if rank is None:
-        return
     cores = list(T.cores)
     S = T.sem
     nev = [0]
@@ -55,6 +55,9 @@ def rank_program(g, core, T, topo):
     def same_chip(a, b):
         return topo.host(a) == topo.host(b) and topo.chip(a) == topo.chip(b)
 
+    if not any(same_chip(core, c) for c in cores):
+        return
+
     def same_side(a, b):
         return same_chip(a, b) or topo.same_plane(a, b)
 
@@ -62,7 +65,7 @@ def rank_program(g, core, T, topo):
     sides = [side0, [c for c in cores if c not in side0]]
 
     def side_of(c):
-        return 0 if c in sides[0] else 1
+        return 0 if any(same_side(c, d) for d in sides[0]) else 1
 
     def has_port(c):
         return all(topo.may_write(c, o) for o in sides[1 - side_of(c)])
@@ -70,8 +73,17 @@ def rank_program(g, core, T, topo):
     NP = [[c for c in s if not has_port(c)] for s in sides]
     PT = [[c for c in s if has_port(c)] for s in sides]
     slots = NP[0] + PT[0] + PT[1] + NP[1]
-    blk_np = [(0, len(NP[0])), (NR - len(NP[1]), NR)]
-    blk_pt = (len(NP[0]), NR - len(NP[1]))
+    a0, a1, a2 = len(NP[0]), len(NP[0]) + len(PT[0]), NR - len(NP[1])
+    prs_np = [list(range(0, a0 // 2)), list(range(a2 // 2, NP2))]
+    prs_pt = [list(range(a0 // 2, a1 // 2)), list(range(a1 // 2, a2 // 2))]
+
+    def forwarders(q):
+        return [c for c in range(max(cores) + 8) if c not in cores and same_chip(c, q)
+                and topo.die(c) == topo.die(q) and has_port(c)]
+
+    def share(q, f):
+        fs = forwarders(q)
+        return sides[1 - side_of(q)][fs.index(f)::len(fs)]
 
     def lo(c):
         o = [d for d in cores if same_side(c, d) and not same_chip(c, d)][0]
@@ -86,16 +98,18 @@ def rank_program(g, core, T, topo):
     def hop1_dsts(c):
         if has_port(c):
             return NP[0] + NP[1]
-        return PT[side_of(c)]
+        return PT[side_of(c)] + forwarders(c)
 
-    def cross_server(d):
-        o = 1 - side_of(d)
-        return PT[o][sides[side_of(d)].index(d) % len(PT[o])]
+    def pcols(js):
+        return T.wall[:, 2 * js[0] * D:(2 * js[-1] + 2) * D]
 
-    def wcols(b):
-        return T.wall[:, b[0] * D:b[1] * D]
+    def scols(s):
+        return T.wall[:, s * D:(s + 1) * D]
 
-    def send(src_ap, dst_ap, dsts, sem):
+    def wsem(j):
+        return S["w%d" % j]
+
+    def fused(src_ap, dst_ap, dsts, sem):
         groups = {}
         for d in dsts:
             groups.setdefault(m1(core, d), []).append(d)
@@ -112,63 +126,88 @@ def rank_program(g, core, T, topo):
         g.remote_dma_fused(trs, local_sem=S.sent)
         return tot
 
+    if rank is None:
+        for q in NP[0] + NP[1]:
+            if core in forwarders(q):
+                s = slots.index(q)
+                g.wait_ge(wsem(s // 2), _n(m1(q, core)))
+                n = fused(scols(s), scols(s), share(q, core), wsem(s // 2))
+                g.wait_ge(S.sent, n)
+        return
+
     me_port = has_port(core)
     sd = side_of(core)
     mate = [c for c in cores if same_chip(c, core) and c != core][0]
-    h1_cnt = sum(_n(m1(q, core)) for q in cores if q != core and core in hop1_dsts(q))
+    my_slot = slots.index(core)
+    pt_pieces = [prs_pt[sd], prs_pt[1 - sd]]
+    pt_order = pt_pieces[0] + pt_pieces[1]
+
+    def h1_cnt(j):
+        return sum(_n(m1(q, core)) for q in slots[2 * j:2 * j + 2] if q != core and core in hop1_dsts(q))
+
+    def fw_cnt(j):
+        return sum(_n(lo(f)) for q in slots[2 * j:2 * j + 2] for f in forwarders(q) if core in share(q, f))
+
+    arr = {}
     if me_port:
-        h2a_cnt = _n(topo.mask(mate, core))
-        order = [(blk_np[sd], S.h1, h1_cnt), (blk_pt, S.h2a, h2a_cnt)]
+        use = prs_np[sd] + pt_order + prs_np[1 - sd]
+        for j in prs_np[sd]:
+            arr[j] = (wsem(j), h1_cnt(j))
+        for piece in pt_pieces:
+            for j in piece:
+                arr[j] = (wsem(piece[0]), _n(topo.mask(mate, core)))
     else:
-        h2a_cnt = _n(m1(mate, core))
-        order = [(blk_pt, S.h1, h1_cnt), (blk_np[sd], S.h2a, h2a_cnt)]
-    order.append((blk_np[1 - sd], S.h2b, _n(lo(cross_server(core)))))
+        use = pt_order + prs_np[sd] + prs_np[1 - sd]
+        for j in pt_order:
+            arr[j] = (wsem(j), h1_cnt(j))
+        for j in prs_np[sd]:
+            arr[j] = (wsem(j), _n(m1(mate, core)))
+    for j in prs_np[1 - sd]:
+        arr[j] = (wsem(j), fw_cnt(j))
+
+    V, PE, A = g.vector, g.tensor, g.scalar
 
     g.sync.dma_start(T.wown[:], T.w[:]).then_inc(S.ld_w, 16)
-    g.scalar.dma_start(T.xx[:, 0:TK], T.x[:]).then_inc(S.ld_in, 16)
-    g.scalar.dma_start(T.rts[:], T.rt[:]).then_inc(S.ld_in, 16)
+    A.dma_start(T.xx[:, 0:TK], T.x[:]).then_inc(S.ld_in, 16)
+    A.dma_start(T.rts[:], T.rt[:]).then_inc(S.ld_in, 16)
     g.sync.dma_start(T.rms[0:NR, :], T.rm[:]).then_inc(S.ld_in, 16)
     g.sync.dma_start(T.xx[:, TK:2 * TK], T.x[:]).then_inc(S.ld_in, 16)
     LD = 64
 
-    e_ones, e_id, e_esel = ev(), ev(), ev()
-    g.vector.memset(T.ones[:], 1.0).then_inc(e_ones, 1)
+    e_ones, e_id, e_esel, e_on2, e_esel2 = ev(), ev(), ev(), ev(), ev()
+    V.memset(T.ones[:], 1.0).then_inc(e_ones, 1)
     g.wait_ge(e_ones, 1)
     g.affine_select(T.ident[:], T.ones[:], [[-1, 128]], AluOpType.is_equal, 0.0, 0, 1).then_inc(e_id, 1)
+    A.wait_ge(e_ones, 1)
+    A.activation(T.ones2[0:NR, :], T.ones[0:NR, :], ActivationFunctionType.Exp, scale=0.0).then_inc(e_on2, 1)
 
     sent = 0
     g.wait_ge(S.ld_w, 16)
-    my_slot = slots.index(core)
-    sent += send(T.wown[:], T.wall[:, my_slot * D:(my_slot + 1) * D], hop1_dsts(core), S.h1)
-    g.wait_ge(S.h1, h1_cnt)
+    sent += fused(T.wown[:], scols(my_slot), hop1_dsts(core), wsem(my_slot // 2))
     if me_port:
-        b = blk_np[sd]
-        far = [d for d in sides[1 - sd] if cross_server(d) == core]
-        groups = [([mate], hi(core, mate), S.h2a), (far, lo(core), S.h2b)]
-        trs = []
-        for ds, m, sem in groups:
-            ids = []
-            for d in ds:
-                rid, pid = topo.addr(d, core)
-                ids.append(DstId(rid=rid, pnc=pid))
-            trs.append(RemoteDMATransfer(dst_ids=ids, dma_engine_mask=m, remote_sem=sem,
-                                         srcs=[wcols(b)], dsts=[wcols(b) for _ in ds], alu_op=0))
-            sent += _n(m)
-        g.remote_dma_fused(trs, local_sem=S.sent)
+        for j in prs_np[sd]:
+            g.wait_ge(arr[j][0], arr[j][1])
+            sent += fused(pcols([j]), pcols([j]), [mate], wsem(j))
     else:
         rid, pid = topo.addr(mate, core)
         m = topo.mask(core, mate)
-        g.remote_dma(wcols(blk_pt), wcols(blk_pt), S.h2a, S.sent, pid, rid, m)
-        sent += _n(m)
+        for piece in pt_pieces:
+            for j in piece:
+                g.wait_ge(arr[j][0], arr[j][1])
+            g.remote_dma(pcols(piece), pcols(piece), wsem(piece[0]), S.sent, pid, rid, m)
+            sent += _n(m)
     g.wait_ge(S.sent, sent)
 
-    V, PE, A = g.vector, g.tensor, g.scalar
+    def esel_blk(s, src, sem):
+        e = T.rank_of(slots[s])
+        V.tensor_scalar(T.esel[0:NR, s * 128:(s + 1) * 128], src[0:NR, :], T.ident[0:NR, e:e + 1], None,
+                        AluOpType.mult).then_inc(sem, 1)
+
     V.wait_ge(e_ones, 1)
     V.wait_ge(e_id, 1)
-    for s in range(NR):
-        e = T.rank_of(slots[s])
-        V.tensor_scalar(T.esel[0:NR, s * 128:(s + 1) * 128], T.ones[0:NR, :], T.ident[0:NR, e:e + 1], None,
-                        AluOpType.mult).then_inc(e_esel, 1)
+    for j in use[:-1]:
+        esel_blk(2 * j, T.ones, e_esel)
+        esel_blk(2 * j + 1, T.ones, e_esel)
 
     e_rmT, e_s = ev(), ev()
     PE.wait_ge(S.ld_in, LD)
@@ -211,21 +250,23 @@ def rank_program(g, core, T, topo):
                   True, True).then_inc(e_gps, 1)
     A.wait_ge(e_gps, 2)
     A.activation(T.gsb[0:NR, :], T.ps_g[0:NR, 0:TK], ActivationFunctionType.Copy).then_inc(e_g, 1)
+    V.wait_ge(e_on2, 1)
+    esel_blk(2 * use[-1], T.ones2, e_esel2)
+    esel_blk(2 * use[-1] + 1, T.ones2, e_esel2)
 
-    pairs = []
-    for b, _, _ in order:
-        pairs += list(range(b[0] // 2, b[1] // 2))
-    e_G = [ev() for _ in pairs]
+    e_G = [ev() for _ in use]
     e_xg = {}
-    for j in pairs:
+    for j in use:
         e_xg[j] = ev()
     PE.wait_ge(e_g, 1)
-    PE.wait_ge(e_esel, NR)
+    PE.wait_ge(e_esel, NR - 2)
     V.wait_ge(S.ld_in, LD)
-    for i, j in enumerate(pairs):
+    for i, j in enumerate(use):
         bank = T["ps_G%d" % (i % NG)]
         if i >= NG:
-            PE.wait_ge(e_xg[pairs[i - NG]], 1)
+            PE.wait_ge(e_xg[use[i - NG]], 1)
+        if i == len(use) - 1:
+            PE.wait_ge(e_esel2, 2)
         for h in range(2):
             s = 2 * j + h
             PE.matmul(bank[:, h * TK:(h + 1) * TK], T.esel[0:NR, s * 128:(s + 1) * 128], T.gsb[0:NR, :],
@@ -234,17 +275,23 @@ def rank_program(g, core, T, topo):
         V.tensor_tensor(T.xg[:, j * 2 * TK:(j + 1) * 2 * TK], T.xx[:], bank[:], AluOpType.mult).then_inc(e_xg[j], 1)
 
     e_y, e_ysb = ev(), ev()
-    k = 0
-    for b, sem, cnt in order:
-        PE.wait_ge(sem, cnt)
-        for s in range(b[0], b[1]):
-            if s % 2 == 0:
-                PE.wait_ge(e_xg[s // 2], 1)
-            mm = PE.matmul(T.ps_y[:, 0:TK], T.wall[:, s * D:(s + 1) * D], T.xg[:, s * TK:(s + 1) * TK],
-                           k == 0, k == NR - 1)
-            k += 1
-            if k == NR:
-                mm.then_inc(e_y, 1)
+    PE.wait_ge(S.ld_w, 16)
+    k = [0]
+
+    def expert(w_ap, s):
+        mm = PE.matmul(T.ps_y[:, 0:TK], w_ap, T.xg[:, s * TK:(s + 1) * TK], k[0] == 0, k[0] == NR - 1)
+        k[0] += 1
+        if k[0] == NR:
+            mm.then_inc(e_y, 1)
+
+    for j in use:
+        PE.wait_ge(e_xg[j], 1)
+        if my_slot // 2 == j:
+            expert(T.wown[:], my_slot)
+        PE.wait_ge(arr[j][0], arr[j][1])
+        for s in (2 * j, 2 * j + 1):
+            if s != my_slot:
+                expert(scols(s), s)
     V.wait_ge(e_y, 1)
     V.tensor_copy(T.ysb[:], T.ps_y[:, 0:TK]).then_inc(e_ysb, 1)
     g.sync.wait_ge(e_ysb, 1)

from concourse.bass import DstId, RemoteDMATransfer
from concourse.mybir import AluOpType, AxisListType, ActivationFunctionType

NR, D, TK = 12, 128, 256
NP2 = NR // 2
NG = 4

SCRATCH = {
    "wown": ("sbuf", [128, D], "bfloat16"),
    "wall": ("sbuf", [128, NR * D], "bfloat16"),
    "xx": ("sbuf", [128, 2 * TK], "bfloat16"),
    "rts": ("sbuf", [128, NR], "bfloat16"),
    "rms": ("sbuf", [128, TK], "bfloat16"),
    "ones": ("sbuf", [128, 128], "bfloat16"),
    "ones2": ("sbuf", [128, 128], "bfloat16"),
    "ident": ("sbuf", [128, 128], "bfloat16"),
    "esel": ("sbuf", [128, NR * 128], "bfloat16"),
    "pen": ("sbuf", [128, 2 * NR], "float32"),
    "sm": ("sbuf", [128, 2 * NR], "float32"),
    "mx": ("sbuf", [128, 4], "float32"),
    "dd": ("sbuf", [128, 2 * NR], "float32"),
    "ex": ("sbuf", [128, 2 * NR], "float32"),
    "ssum": ("sbuf", [128, 4], "float32"),
    "rs": ("sbuf", [128, 4], "float32"),
    "gt": ("sbuf", [128, 2 * NR], "bfloat16"),
    "gsb": ("sbuf", [128, TK], "bfloat16"),
    "xg": ("sbuf", [128, NR * TK], "bfloat16"),
    "ysb": ("sbuf", [128, TK], "bfloat16"),
    "ps_s": ("psum", [128, 512], "float32"),
    "ps_rm": ("psum", [128, 512], "float32"),
    "ps_g": ("psum", [128, 512], "float32"),
    "ps_G0": ("psum", [128, 512], "float32"),
    "ps_G1": ("psum", [128, 512], "float32"),
    "ps_G2": ("psum", [128, 512], "float32"),
    "ps_G3": ("psum", [128, 512], "float32"),
    "ps_y": ("psum", [128, 512], "float32"),
}
SEMAPHORES = ["ld_w", "ld_in", "sent", "st"] + ["w%d" % i for i in range(NP2)] + ["e%d" % i for i in range(44)]


def _n(mask):
    return bin(mask).count("1")


def rank_program(g, core, T, topo):
    rank = T.rank_of(core)
    cores = list(T.cores)
    S = T.sem
    nev = [0]

    def ev():
        nev[0] += 1
        return S["e%d" % (nev[0] - 1)]

    def same_chip(a, b):
        return topo.host(a) == topo.host(b) and topo.chip(a) == topo.chip(b)

    if not any(same_chip(core, c) for c in cores):
        return

    def same_side(a, b):
        return same_chip(a, b) or topo.same_plane(a, b)

    side0 = [c for c in cores if same_side(c, cores[0])]
    sides = [side0, [c for c in cores if c not in side0]]

    def side_of(c):
        return 0 if any(same_side(c, d) for d in sides[0]) else 1

    def has_port(c):
        return all(topo.may_write(c, o) for o in sides[1 - side_of(c)])

    NP = [[c for c in s if not has_port(c)] for s in sides]
    PT = [[c for c in s if has_port(c)] for s in sides]
    slots = NP[0] + PT[0] + PT[1] + NP[1]
    a0, a1, a2 = len(NP[0]), len(NP[0]) + len(PT[0]), NR - len(NP[1])
    prs_np = [list(range(0, a0 // 2)), list(range(a2 // 2, NP2))]
    prs_pt = [list(range(a0 // 2, a1 // 2)), list(range(a1 // 2, a2 // 2))]

    def forwarders(q):
        return [c for c in range(max(cores) + 8) if c not in cores and same_chip(c, q)
                and topo.die(c) == topo.die(q) and has_port(c)]

    def share(q, f):
        fs = forwarders(q)
        return sides[1 - side_of(q)][fs.index(f)::len(fs)]

    def lo(c):
        o = [d for d in cores if same_side(c, d) and not same_chip(c, d)][0]
        return topo.mask(c, o)

    def hi(c, d):
        return topo.mask(c, d) & ~lo(c)

    def m1(c, d):
        return hi(c, d) if same_chip(c, d) else lo(c)

    def hop1_dsts(c):
        if has_port(c):
            return NP[0] + NP[1]
        return PT[side_of(c)] + forwarders(c)

    def pcols(js):
        return T.wall[:, 2 * js[0] * D:(2 * js[-1] + 2) * D]

    def scols(s):
        return T.wall[:, s * D:(s + 1) * D]

    def wsem(j):
        return S["w%d" % j]

    def fused(src_ap, dst_ap, dsts, sem):
        groups = {}
        for d in dsts:
            groups.setdefault(m1(core, d), []).append(d)
        trs = []
        tot = 0
        for m, ds in groups.items():
            ids = []
            for d in ds:
                rid, pid = topo.addr(d, core)
                ids.append(DstId(rid=rid, pnc=pid))
            trs.append(RemoteDMATransfer(dst_ids=ids, dma_engine_mask=m, remote_sem=sem,
                                         srcs=[src_ap], dsts=[dst_ap for _ in ds], alu_op=0))
            tot += _n(m)
        g.remote_dma_fused(trs, local_sem=S.sent)
        return tot

    if rank is None:
        for q in NP[0] + NP[1]:
            if core in forwarders(q):
                s = slots.index(q)
                g.wait_ge(wsem(s // 2), _n(m1(q, core)))
                n = fused(scols(s), scols(s), share(q, core), wsem(s // 2))
                g.wait_ge(S.sent, n)
        return

    me_port = has_port(core)
    sd = side_of(core)
    mate = [c for c in cores if same_chip(c, core) and c != core][0]
    my_slot = slots.index(core)
    pt_pieces = [prs_pt[sd], prs_pt[1 - sd]]
    pt_order = pt_pieces[0] + pt_pieces[1]

    def h1_cnt(j):
        return sum(_n(m1(q, core)) for q in slots[2 * j:2 * j + 2] if q != core and core in hop1_dsts(q))

    def fw_cnt(j):
        return sum(_n(lo(f)) for q in slots[2 * j:2 * j + 2] for f in forwarders(q) if core in share(q, f))

    arr = {}
    if me_port:
        use = prs_np[sd] + pt_order + prs_np[1 - sd]
        for j in prs_np[sd]:
            arr[j] = (wsem(j), h1_cnt(j))
        for piece in pt_pieces:
            for j in piece:
                arr[j] = (wsem(piece[0]), _n(topo.mask(mate, core)))
    else:
        use = pt_order + prs_np[sd] + prs_np[1 - sd]
        for j in pt_order:
            arr[j] = (wsem(j), h1_cnt(j))
        for j in prs_np[sd]:
            arr[j] = (wsem(j), _n(m1(mate, core)))
    for j in prs_np[1 - sd]:
        arr[j] = (wsem(j), fw_cnt(j))

    V, PE, A = g.vector, g.tensor, g.scalar

    g.sync.dma_start(T.wown[:], T.w[:]).then_inc(S.ld_w, 16)
    A.dma_start(T.xx[:, 0:TK], T.x[:]).then_inc(S.ld_in, 16)
    A.dma_start(T.rts[:], T.rt[:]).then_inc(S.ld_in, 16)
    g.sync.dma_start(T.rms[0:NR, :], T.rm[:]).then_inc(S.ld_in, 16)
    g.sync.dma_start(T.xx[:, TK:2 * TK], T.x[:]).then_inc(S.ld_in, 16)
    LD = 64

    e_ones, e_id, e_esel, e_on2, e_esel2 = ev(), ev(), ev(), ev(), ev()
    V.memset(T.ones[:], 1.0).then_inc(e_ones, 1)
    g.wait_ge(e_ones, 1)
    g.affine_select(T.ident[:], T.ones[:], [[-1, 128]], AluOpType.is_equal, 0.0, 0, 1).then_inc(e_id, 1)
    A.wait_ge(e_ones, 1)
    A.activation(T.ones2[0:NR, :], T.ones[0:NR, :], ActivationFunctionType.Exp, scale=0.0).then_inc(e_on2, 1)

    sent = 0
    g.wait_ge(S.ld_w, 16)
    sent += fused(T.wown[:], scols(my_slot), hop1_dsts(core), wsem(my_slot // 2))
    if me_port:
        for j in prs_np[sd]:
            g.wait_ge(arr[j][0], arr[j][1])
            sent += fused(pcols([j]), pcols([j]), [mate], wsem(j))
    else:
        rid, pid = topo.addr(mate, core)
        m = topo.mask(core, mate)
        for piece in pt_pieces:
            for j in piece:
                g.wait_ge(arr[j][0], arr[j][1])
            g.remote_dma(pcols(piece), pcols(piece), wsem(piece[0]), S.sent, pid, rid, m)
            sent += _n(m)
    g.wait_ge(S.sent, sent)

    def esel_blk(s, src, sem):
        e = T.rank_of(slots[s])
        V.tensor_scalar(T.esel[0:NR, s * 128:(s + 1) * 128], src[0:NR, :], T.ident[0:NR, e:e + 1], None,
                        AluOpType.mult).then_inc(sem, 1)

    V.wait_ge(e_ones, 1)
    V.wait_ge(e_id, 1)
    for j in use[:-1]:
        esel_blk(2 * j, T.ones, e_esel)
        esel_blk(2 * j + 1, T.ones, e_esel)

    e_rmT, e_s = ev(), ev()
    PE.wait_ge(S.ld_in, LD)
    PE.wait_ge(e_id, 1)
    for b in range(2):
        PE.matmul(T.ps_rm[:, b * NR:(b + 1) * NR], T.rms[0:NR, b * 128:(b + 1) * 128], T.ident[0:NR, 0:NR],
                  True, True).then_inc(e_rmT, 1)
    for b in range(2):
        PE.matmul(T.ps_s[:, b * NR:(b + 1) * NR], T.xx[:, b * 128:(b + 1) * 128], T.rts[:],
                  True, True).then_inc(e_s, 1)

    e_p1, e_p2, e_sm, e_m, e_d, e_ex, e_r, e_gt, e_gps, e_g = [ev() for _ in range(10)]
    V.wait_ge(e_rmT, 2)
    V.tensor_scalar(T.pen[:], T.ps_rm[:, 0:2 * NR], -0.5, 1e29, AluOpType.add, AluOpType.mult).then_inc(e_p1, 1)
    V.wait_ge(e_p1, 1)
    V.tensor_scalar(T.pen[:], T.pen[:], 1e9, None, AluOpType.mult).then_inc(e_p2, 1)
    V.wait_ge(e_p2, 1)
    V.wait_ge(e_s, 2)
    V.tensor_tensor(T.sm[:], T.ps_s[:, 0:2 * NR], T.pen[:], AluOpType.min).then_inc(e_sm, 1)
    V.wait_ge(e_sm, 1)
    for b in range(2):
        V.tensor_reduce(T.mx[:, b:b + 1], T.sm[:, b * NR:(b + 1) * NR], AxisListType.X, AluOpType.max).then_inc(e_m, 1)
    V.wait_ge(e_m, 2)
    for b in range(2):
        V.tensor_scalar(T.dd[:, b * NR:(b + 1) * NR], T.sm[:, b * NR:(b + 1) * NR], T.mx[:, b:b + 1], -200.0,
                        AluOpType.subtract, AluOpType.max).then_inc(e_d, 1)
    A.wait_ge(e_d, 2)
    for b in range(2):
        A.activation(T.ex[:, b * NR:(b + 1) * NR], T.dd[:, b * NR:(b + 1) * NR], ActivationFunctionType.Exp,
                     accum_out=T.ssum[:, b:b + 1]).then_inc(e_ex, 1)
    V.wait_ge(e_ex, 2)
    V.reciprocal(T.rs[:, 0:2], T.ssum[:, 0:2]).then_inc(e_r, 1)
    V.wait_ge(e_r, 1)
    for b in range(2):
        V.tensor_scalar(T.gt[:, b * NR:(b + 1) * NR], T.ex[:, b * NR:(b + 1) * NR], T.rs[:, b:b + 1], None,
                        AluOpType.mult).then_inc(e_gt, 1)
    PE.wait_ge(e_gt, 2)
    for b in range(2):
        PE.matmul(T.ps_g[0:NR, b * 128:(b + 1) * 128], T.gt[:, b * NR:(b + 1) * NR], T.ident[:],
                  True, True).then_inc(e_gps, 1)
    A.wait_ge(e_gps, 2)
    A.activation(T.gsb[0:NR, :], T.ps_g[0:NR, 0:TK], ActivationFunctionType.Copy).then_inc(e_g, 1)
    V.wait_ge(e_on2, 1)
    esel_blk(2 * use[-1], T.ones2, e_esel2)
    esel_blk(2 * use[-1] + 1, T.ones2, e_esel2)

    e_G = [ev() for _ in use]
    e_xg = {}
    for j in use:
        e_xg[j] = ev()
    PE.wait_ge(e_g, 1)
    PE.wait_ge(e_esel, NR - 2)
    V.wait_ge(S.ld_in, LD)
    for i, j in enumerate(use):
        bank = T["ps_G%d" % (i % NG)]
        if i >= NG:
            PE.wait_ge(e_xg[use[i - NG]], 1)
        if i == len(use) - 1:
            PE.wait_ge(e_esel2, 2)
        for h in range(2):
            s = 2 * j + h
            PE.matmul(bank[:, h * TK:(h + 1) * TK], T.esel[0:NR, s * 128:(s + 1) * 128], T.gsb[0:NR, :],
                      True, True).then_inc(e_G[i], 1)
        V.wait_ge(e_G[i], 2)
        V.tensor_tensor(T.xg[:, j * 2 * TK:(j + 1) * 2 * TK], T.xx[:], bank[:], AluOpType.mult).then_inc(e_xg[j], 1)

    e_y, e_ysb = ev(), ev()
    PE.wait_ge(S.ld_w, 16)
    k = [0]

    def expert(w_ap, s):
        mm = PE.matmul(T.ps_y[:, 0:TK], w_ap, T.xg[:, s * TK:(s + 1) * TK], k[0] == 0, k[0] == NR - 1)
        k[0] += 1
        if k[0] == NR:
            mm.then_inc(e_y, 1)

    for j in use:
        PE.wait_ge(e_xg[j], 1)
        if my_slot // 2 == j:
            expert(T.wown[:], my_slot)
        PE.wait_ge(arr[j][0], arr[j][1])
        for s in (2 * j, 2 * j + 1):
            if s != my_slot:
                expert(scols(s), s)
    V.wait_ge(e_y, 1)
    V.tensor_copy(T.ysb[:], T.ps_y[:, 0:TK]).then_inc(e_ysb, 1)
    g.sync.wait_ge(e_ysb, 1)
    g.sync.dma_start(T.y[:], T.ysb[:]).then_inc(S.st, 16)
    g.sync.wait_ge(S.st, 16)
